import numpy as np
import ml_dtypes


def mxq(x, axis, fmt="e4m3"):
    dtype, down = {"e4m3": (ml_dtypes.float8_e4m3fn, 7), "e5m2": (ml_dtypes.float8_e5m2, 14)}[fmt]
    v = np.moveaxis(np.asarray(x, np.float32).astype(ml_dtypes.bfloat16).astype(np.float64), axis, -1)
    blocks = v.reshape(v.shape[:-1] + (-1, 32))
    amax = np.abs(blocks).max(-1, keepdims=True)
    byte = np.maximum(np.where(amax > 0, np.frexp(amax)[1] - 1 + 127, 0) - down, 1)
    scale = np.exp2(byte - 127.0)
    codes = (blocks / scale).astype(np.float32).astype(dtype).astype(np.float64)
    return np.moveaxis((codes * scale).reshape(v.shape), -1, axis)


WIDE = False


def mx_kscale(k):
    if not WIDE:
        return np.ones(k)
    levels = np.array([10, -10, 5, -5, 0])
    if k % 512:
        return np.exp2(np.random.permutation(np.resize(levels, k // 32))).repeat(32)
    a = np.empty((k // 512, 16))
    for p in range(k // 512):
        a[p, :8] = np.random.permutation(np.resize(levels, 8))
        for g in range(8):
            far = levels[np.abs(levels - a[p, g]) >= 10]
            a[p, g + 8] = far[np.random.randint(len(far))]
    return np.exp2(a.ravel()).repeat(32)


def f64(x):
    return np.asarray(x).astype(np.float64)


def striped(idx):
    return np.tile(idx.reshape(-1, 16).T, (8, 1)).astype(np.uint16)


def unstriped(offs):
    return offs[:16].T.reshape(-1).astype(np.int64)


def pack_weight(w):
    k, n = w.shape
    w = f64(np.asarray(w, np.float32).astype(ml_dtypes.bfloat16)).reshape(k // 32, 32, n)
    amax = np.abs(w).max(1)
    byte = np.clip(np.where(amax > 0, np.frexp(amax)[1] - 1 + 127 - 7, 1), 1, 254)
    scaled = (w * np.exp2(127.0 - byte)[:, None, :]).reshape(k, n).astype(np.float32)
    words = np.ascontiguousarray(scaled.reshape(k // 512, 128, 4, n).transpose(0, 1, 3, 2)).astype(ml_dtypes.float8_e4m3fn).view(np.uint8)
    return words, np.ascontiguousarray(byte.astype(np.uint8).reshape(k // 512, 16, n))


def unpack_weight(words, scales):
    g, p, n, _ = words.shape
    vals = np.ascontiguousarray(words).view(ml_dtypes.float8_e4m3fn).astype(np.float64) * np.repeat(np.exp2(scales.astype(np.float64) - 127.0), 8, axis=1)[..., None]
    return vals.transpose(0, 1, 3, 2).reshape(g * 512, n)


E2M1 = np.array([0.0, 0.5, 1.0, 1.5, 2.0, 3.0, 4.0, 6.0, -0.0, -0.5, -1.0, -1.5, -2.0, -3.0, -4.0, -6.0])


def pack_fp4(w):
    k, n = w.shape
    w = f64(np.asarray(w, np.float32).astype(ml_dtypes.bfloat16)).reshape(k // 32, 32, n)
    amax = np.abs(w).max(1)
    mant, ex = np.frexp(amax / 6.0)
    byte = np.clip(np.where(amax > 0, np.where(mant > 0.5, ex, ex - 1) + 127, 1), 1, 254)
    scaled = (w * np.exp2(127.0 - byte)[:, None, :]).reshape(k, n).astype(np.float32)
    c = np.ascontiguousarray(scaled.reshape(k // 512, 128, 4, n).transpose(0, 1, 3, 2)).astype(ml_dtypes.float4_e2m1fn).view(np.uint8) & 0xF
    words = (c[..., 0::2] | (c[..., 1::2] << 4)).reshape(k // 512, 128, 2 * n)
    return np.ascontiguousarray(words), np.ascontiguousarray(byte.astype(np.uint8).reshape(k // 512, 16, n))


def unpack_fp4(words, scales):
    g, _, n = scales.shape
    words = np.ascontiguousarray(words).reshape(g, 128, n, 2)
    nib = np.empty((g, 128, n, 4), np.uint8)
    nib[..., 0::2] = words & 0xF
    nib[..., 1::2] = words >> 4
    vals = E2M1[nib] * np.repeat(np.exp2(scales.astype(np.float64) - 127.0), 8, axis=1)[..., None]
    return vals.transpose(0, 1, 3, 2).reshape(g * 512, n)


def sigmoid(v):
    return 1.0 / (1.0 + np.exp(-np.maximum(v, -700.0)))


K, T, S, D, N, H, V, U = 512, 2048, 1024, 4, 256, 512, 256, 512


def setup_inputs():
    n = np.random.standard_normal
    s = mx_kscale(K)[:, None]
    u = mx_kscale(H)
    packed_xT = pack_weight(n((K, T)) * s)
    packed_w1 = pack_fp4(n((K, H)) / np.sqrt(K) / s)
    packed_w2 = pack_fp4(n((H, N)) / np.sqrt(H) / u[:, None])
    return {
        "x_words": packed_xT[0],
        "x_scales": packed_xT[1],
        "w1_words": packed_w1[0],
        "w1_scales": packed_w1[1],
        "qry": (n((H, S))).astype(np.float32),
        "unit": (np.random.uniform(0.6, 1.4, (H, 1)) * u[:, None]).astype(np.float32),
        "w2_words": packed_w2[0],
        "w2_scales": packed_w2[1],
        "offs": striped(np.random.permutation(T)[:S]),
        "hop": striped(np.random.permutation(S)),
        "cand": striped(np.random.permutation(np.concatenate([np.arange(V), np.random.randint(0, V, U - V)]))),
    }


def reference(x_words, x_scales, w1_words, w1_scales, qry, unit, w2_words, w2_scales, offs, hop, cand):
    xq = unpack_weight(x_words, x_scales)[:, unstriped(offs)]
    y = unpack_fp4(w1_words, w1_scales).T @ xq
    yh = y[:, unstriped(hop)]
    dn = (y - yh) ** 2
    dq = (y - f64(qry)) ** 2
    kept_ = sigmoid(1.5 * (dn - (0.8 * dq)))
    kd = kept_ * (np.exp(-1.0 * np.sqrt(dq + 0.05)))
    rank = kd.reshape(len(kd), -1, D).sum(axis=2)
    rc = rank[:, unstriped(cand)]
    best = dq.reshape(len(dq), -1, D).min(axis=2)
    mc = best[:, unstriped(cand)]
    hid = f64(unit) * (rc / (mc + 0.5))
    return unpack_fp4(w2_words, w2_scales).T @ mxq(hid, 0, "e4m3")

@@ -1,0 +1,236 @@
+from contextlib import ExitStack
+
+import concourse.mybir as mybir
+from concourse.masks import make_identity
+
+F32 = mybir.dt.float32
+BF16 = mybir.dt.bfloat16
+I32 = mybir.dt.int32
+U32 = mybir.dt.uint32
+U16 = mybir.dt.uint16
+U8 = mybir.dt.uint8
+FP8X4 = mybir.dt.float8_e4m3fn_x4
+FP4X4 = mybir.dt.float4_e2m1fn_x4
+ALU = mybir.AluOpType
+ACT = mybir.ActivationFunctionType
+
+P = 128
+PACK = 4
+T, S, H, N, V, U, D = 2048, 1024, 512, 256, 256, 512, 4
+BANK = 512
+FLOPS = 2 * 512 * H * S + 2 * H * N * U
+
+
+def load_scale_rows(nc, plane, scales):
+    for q in range(4):
+        nc.sync.dma_start(out=plane[32 * q : 32 * q + 4, :].bitcast(I32), in_=scales[0, 4 * q : 4 * q + 4, :].bitcast(I32))
+
+
+def tile_picked_yhnswp_rel_p_kernel(
+    tc, x_words, x_scales, w1_words, w1_scales, qry, unit, w2_words, w2_scales, offs, hop, cand, out
+):
+    nc = tc.nc
+    with ExitStack() as ctx:
+        keep = ctx.enter_context(tc.tile_pool(name="keep", bufs=1))
+        psum = ctx.enter_context(tc.psum_pool(name="psum", bufs=1))
+
+        offs_sb = keep.tile([P, S // 16], U16, name="offs_sb")
+        hop_sb = keep.tile([P, S // 16], U16, name="hop_sb")
+        cand_sb = keep.tile([P, U // 16], U16, name="cand_sb")
+        x_tab = keep.tile([P, T], I32, name="x_tab", align_bytes=64)
+        xs_tab = keep.tile([P, T], U8, name="xs_tab", align_bytes=64)
+        w1_raw = keep.tile([P, 2 * H], U8, name="w1_raw", align_bytes=64)
+        w1s_raw = keep.tile([P, H], U8, name="w1s_raw", align_bytes=64)
+        w1_sb = keep.tile([P, 2 * H], U8, name="w1_sb", align_bytes=64)
+        w1s_sb = keep.tile([P, H], U8, name="w1s_sb", align_bytes=64)
+        w2_sb = keep.tile([P, 2 * N], U8, name="w2_sb", align_bytes=64)
+        w2s_sb = keep.tile([P, N], U8, name="w2s_sb", align_bytes=64)
+        unit_sb = keep.tile([P, PACK], F32, name="unit_sb")
+        q_sb = [keep.tile([P, S], F32, name="q%d" % t) for t in range(PACK)]
+
+        nc.gpsimd.memset(xs_tab[:].bitcast(I32), 0)
+        nc.gpsimd.memset(w1s_raw[:].bitcast(I32), 0)
+        nc.gpsimd.memset(w2s_sb[:].bitcast(I32), 0)
+
+        ident = keep.tile([P, P], F32, name="ident")
+        make_identity(nc, ident[:])
+
+        nc.sync.dma_start(offs_sb[:], offs)
+        nc.sync.dma_start(out=w1_raw[:].bitcast(I32), in_=w1_words[0].bitcast(I32))
+        nc.sync.dma_start(hop_sb[:], hop)
+        load_scale_rows(nc, xs_tab, x_scales)
+        nc.sync.dma_start(out=x_tab[:], in_=x_words[0].rearrange("p n r -> p (n r)").bitcast(I32))
+        load_scale_rows(nc, w1s_raw, w1_scales)
+        q_rows = qry.rearrange("(p t) j -> p t j", t=PACK)
+        for t in range(PACK):
+            nc.sync.dma_start(out=q_sb[t][:], in_=q_rows[:, t, :])
+        nc.sync.dma_start(cand_sb[:], cand)
+        nc.sync.dma_start(out=unit_sb[:], in_=unit.rearrange("(p t) o -> p (t o)", t=PACK))
+        nc.sync.dma_start(out=w2_sb[:].bitcast(I32), in_=w2_words[0].bitcast(I32))
+        load_scale_rows(nc, w2s_sb, w2_scales)
+
+        nc.gpsimd.tensor_copy(
+            out=w1_sb[:].rearrange("p (t m b) -> p t m b", t=PACK, b=2),
+            in_=w1_raw[:].rearrange("p (m t b) -> p t m b", t=PACK, b=2),
+        )
+        xg = [keep.tile([P, BANK], U32, name="xg%d" % h, align_bytes=64) for h in range(2)]
+        xsg = [keep.tile([P, BANK], U8, name="xsg%d" % h, align_bytes=64) for h in range(2)]
+        cols = BANK // 16
+        nc.vector.tensor_copy(xsg[0][:], xs_tab[:].indirect(offs_sb[:, 0:cols]))
+        nc.vector.tensor_copy(xg[0][:], x_tab[:].bitcast(U32).indirect(offs_sb[:, 0:cols]))
+        nc.gpsimd.tensor_copy(
+            out=w1s_sb[:].rearrange("p (t m) -> p t m", t=PACK),
+            in_=w1s_raw[:].rearrange("p (m t) -> p t m", t=PACK),
+        )
+        nc.vector.tensor_copy(xsg[1][:], xs_tab[:].indirect(offs_sb[:, cols : 2 * cols]))
+        nc.vector.tensor_copy(xg[1][:], x_tab[:].bitcast(U32).indirect(offs_sb[:, cols : 2 * cols]))
+
+        y_sb = [keep.tile([P, S], F32, name="y%d" % t) for t in range(PACK)]
+        y_twin = [keep.tile([P, S], F32, name="ytwin%d" % t) for t in range(PACK)]
+        to_q = keep.tile([P, PACK, S], F32, name="to_q")
+        to_n = keep.tile([P, PACK, S], F32, name="to_n")
+        dq = keep.tile([P, PACK, 2, D, P], F32, name="dq")
+        ndn = keep.tile([P, PACK, 2, D, P], F32, name="ndn")
+        root = [keep.tile([P, S], F32, name="root%d" % t) for t in range(PACK)]
+        decay = keep.tile([P, PACK, 2, BANK], F32, name="decay")
+        kd = [keep.tile([P, S], F32, name="kd%d" % t) for t in range(PACK)]
+        inv = keep.tile([P, PACK, V], F32, name="inv")
+        pairs = keep.tile([P, PACK, 2, 2, P], F32, name="pairs")
+
+        def bank(t, h, shape, name):
+            return psum.tile(shape, F32, name=name, tag="bank%d" % (2 * t + h))
+
+        def turn(dst, sources):
+            for n, src in enumerate(sources):
+                nc.tensor.matmul(dst, src, ident[:], start=(n == 0), stop=(n == len(sources) - 1), is_transpose=True)
+
+        accs = {}
+        units = [(0, 0), (1, 0), (2, 0), (0, 1), (1, 1), (3, 0), (2, 1), (3, 1)]
+        for t, h in units:
+            half = slice(h * BANK, (h + 1) * BANK)
+            if True:
+                acc = bank(t, h, [P, BANK], "acc")
+                nc.tensor.matmul_mx(
+                    out=acc[:],
+                    lhsT=w1_sb[:, 2 * P * t : 2 * P * (t + 1)].bitcast(FP4X4),
+                    lhsT_scale=w1s_sb[:, P * t : P * (t + 1)],
+                    rhs=xg[h][:].bitcast(FP8X4),
+                    rhs_scale=xsg[h][:],
+                    start=True,
+                    stop=True,
+                )
+                nc.scalar.copy(y_sb[t][:, half], acc[:])
+                accs[t, h] = acc
+                if h == 1:
+                    nc.sync.dma_start(out=y_twin[t][:], in_=y_sb[t][:])
+
+        def neighbour(t):
+            for h in range(2):
+                half = slice(h * BANK, (h + 1) * BANK)
+                nc.vector.tensor_tensor(
+                    to_n[:, t, half], y_sb[t][:].indirect(hop_sb[:, h * cols : (h + 1) * cols]), y_twin[t][:, half], ALU.subtract
+                )
+
+        for t, h in units:
+            if True:
+                half = slice(h * BANK, (h + 1) * BANK)
+                nc.vector.tensor_tensor(to_q[:, t, half], accs[t, h][:], q_sb[t][:, half], ALU.subtract)
+                src = to_q[:, t, half].rearrange("p (v d) -> p v d", d=D)
+                if (t, h) in units[-2:]:
+                    nc.vector.tensor_tensor(dq[:, t, h].rearrange("p d v -> p v d"), src, src, ALU.mult)
+                else:
+                    nc.scalar.activation(dq[:, t, h].rearrange("p d v -> p v d"), src, ACT.Square)
+        for t, h in units:
+            if True:
+                turned = bank(t, h, [P, D, P], "dq_turned")
+                for d in range(D):
+                    turn(turned[:, d, :], [dq[:, t, h, d, :]])
+                nc.scalar.activation(root[t][:, (1 - h) * BANK : (2 - h) * BANK], turned[:].rearrange("p d i -> p (d i)"), ACT.Sqrt, bias=0.05)
+        for t in range(PACK):
+            nc.vector.tensor_tensor(pairs[:, t], dq[:, t, :, 0:2, :], dq[:, t, :, 2:4, :], ALU.min)
+            if t > 0:
+                nc.vector.tensor_tensor(decay[:, t - 1, :, 0:P], pairs[:, t - 1, :, 0, :], pairs[:, t - 1, :, 1, :], ALU.min)
+        neighbour(0)
+        nc.vector.tensor_tensor(decay[:, 3, :, 0:P], pairs[:, 3, :, 0, :], pairs[:, 3, :, 1, :], ALU.min)
+        best = decay[:, :, :, 0:P].rearrange("p t h v -> p (t h) v")
+        inv_units = inv[:].rearrange("p t (h v) -> p (t h) v", h=2)
+        nc.scalar.activation(inv_units, best, ACT.Ln, bias=1.0, scale=2.0)
+        nc.scalar.activation(inv[:], inv[:], ACT.Exp, scale=-1.0)
+
+        picked_all = [keep.tile([P, PACK, U // 2], BF16, name="pickedall%d" % r, align_bytes=64) for r in range(2)]
+        rcols = U // 32
+
+        gaps = {}
+
+        def gap(t):
+            for h in range(2):
+                src = to_n[:, t, h * BANK : (h + 1) * BANK].rearrange("p (v d) -> p v d", d=D)
+                nc.vector.scalar_tensor_tensor(ndn[:, t, h].rearrange("p d v -> p v d"), src, -1.25, src, ALU.mult, ALU.mult)
+                gaps[t, h] = bank(t, h, [P, D, P], "gap")
+                for d in range(D):
+                    turn(gaps[t, h][:, d, :], [dq[:, t, h, d, :], ndn[:, t, h, d, :]])
+
+        def pick(t, r, on_vector):
+            window = windows[t][:].indirect(cand_sb[:, r * rcols : (r + 1) * rcols])
+            if on_vector:
+                nc.vector.tensor_copy(picked_all[r][:, t, :], window)
+            else:
+                nc.scalar.activation(picked_all[r][:, t, :], window, ACT.Copy)
+
+        gap(0)
+        for t in range(1, PACK):
+            neighbour(t)
+            gap(t)
+        windows = root[1:] + [kd[PACK - 1]]
+
+        def ratio(t, ranks):
+            for h in range(2):
+                vs = slice(h * P, (h + 1) * P)
+                nc.vector.scalar_tensor_tensor(windows[t][:, vs], ranks[h][:], unit_sb[:, t : t + 1], inv[:, t, vs], ALU.mult, ALU.mult)
+
+        last = None
+        for t in range(PACK):
+            for h in range(2):
+                nc.scalar.activation(decay[:, t, h, :], root[t][:, (1 - h) * BANK : (2 - h) * BANK], ACT.Exp, scale=-1.0)
+            ranks = []
+            for h in range(2):
+                half = slice(h * BANK, (h + 1) * BANK)
+                nc.scalar.activation(root[t][:, (1 - h) * BANK : (2 - h) * BANK], gaps[t, h][:].rearrange("p d i -> p (d i)"), ACT.Tanh, scale=-0.6)
+                nc.vector.scalar_tensor_tensor(kd[t][:, half], root[t][:, (1 - h) * BANK : (2 - h) * BANK], 1.0, decay[:, t, h, :], ALU.add, ALU.mult)
+                ranks.append(bank(t, h, [P, P], "rank"))
+                turn(ranks[h][:], [kd[t][:, h * BANK + d * P : h * BANK + (d + 1) * P] for d in range(D)])
+            if t > 0:
+                ratio(t - 1, last)
+            last = ranks
+        ratio(PACK - 1, last)
+        for t in range(PACK):
+            for r in range(2):
+                pick(t, r, t >= 2 and r == 0)
+
+        for r in range(2):
+            hid = keep.tile([P, U // 2, PACK], BF16, name="hid%d" % r, align_bytes=64)
+            codes = keep.tile([P, U // 2], U32, name="codes%d" % r, align_bytes=64)
+            hs = keep.tile([P, U // 2], U8, name="hs%d" % r, align_bytes=64)
+            nc.vector.tensor_copy(out=hid[:], in_=picked_all[r][:].rearrange("p t r -> p r t"))
+            nc.vector.quantize_mx(out=codes[:].bitcast(FP8X4), scales=hs[:], in_=hid[:].rearrange("p r t -> p (r t)"))
+            for a in range(2):
+                acc = psum.tile([P, U // 2], F32, name="acc2", tag="bank%d" % (2 * r + a))
+                nc.tensor.matmul_mx(
+                    out=acc[:],
+                    lhsT=w2_sb[:, 2 * P * a : 2 * P * (a + 1)].bitcast(FP4X4),
+                    lhsT_scale=w2s_sb[:, P * a : P * (a + 1)],
+                    rhs=codes[:].bitcast(FP8X4),
+                    rhs_scale=hs[:],
+                    start=True,
+                    stop=True,
+                )
+                res = keep.tile([P, U // 2], F32, name="res%d_%d" % (r, a))
+                dst = out[a * P : (a + 1) * P, r * (U // 2) : (r + 1) * (U // 2)]
+                if r == 1 and a == 1:
+                    nc.vector.tensor_copy(res[:], acc[:])
+                else:
+                    nc.scalar.copy(res[:], acc[:])
+                if r == 1 and a == 0:
+                    nc.scalar.dma_start(out=dst, in_=res[:])
+                else:
+                    nc.sync.dma_start(out=dst, in_=res[:])

@@ -18,6 +18,14 @@ P = 128
 PACK = 4
 T, S, H, N, V, U, D = 2048, 1024, 512, 256, 256, 512, 4
 BANK = 512
+NSQ = 1
+WARM = 1
+VP = ((2, 0), (3, 0))
+SIL = (2, 3)
+SPLIT = 1
+LEAD = 0
+RC = 4
+PRE = 1
 FLOPS = 2 * 512 * H * S + 2 * H * N * U
 
 
@@ -55,6 +63,9 @@ def tile_picked_yhnswp_rel_p_kernel(
         ident = keep.tile([P, P], F32, name="ident")
         make_identity(nc, ident[:])
 
+        if WARM:
+            warm = keep.tile([P, 1], F32, name="warm")
+            nc.scalar.activation(warm[:], w2s_sb[:, 0:4].bitcast(F32), ACT.Sqrt)
         nc.sync.dma_start(offs_sb[:], offs)
         nc.sync.dma_start(out=w1_raw[:].bitcast(I32), in_=w1_words[0].bitcast(I32))
         nc.sync.dma_start(hop_sb[:], hop)
@@ -69,20 +80,21 @@ def tile_picked_yhnswp_rel_p_kernel(
         nc.sync.dma_start(out=w2_sb[:].bitcast(I32), in_=w2_words[0].bitcast(I32))
         load_scale_rows(nc, w2s_sb, w2_scales)
 
-        nc.gpsimd.tensor_copy(
+        nc.vector.tensor_copy(
             out=w1_sb[:].rearrange("p (t m b) -> p t m b", t=PACK, b=2),
             in_=w1_raw[:].rearrange("p (m t b) -> p t m b", t=PACK, b=2),
         )
-        xg = [keep.tile([P, BANK], U32, name="xg%d" % h, align_bytes=64) for h in range(2)]
+        xg = [keep.tile([P, BANK], U32, name="xg0", align_bytes=64)]
         xsg = [keep.tile([P, BANK], U8, name="xsg%d" % h, align_bytes=64) for h in range(2)]
         cols = BANK // 16
         nc.vector.tensor_copy(xsg[0][:], xs_tab[:].indirect(offs_sb[:, 0:cols]))
         nc.vector.tensor_copy(xg[0][:], x_tab[:].bitcast(U32).indirect(offs_sb[:, 0:cols]))
-        nc.gpsimd.tensor_copy(
+        nc.vector.tensor_copy(
             out=w1s_sb[:].rearrange("p (t m) -> p t m", t=PACK),
             in_=w1s_raw[:].rearrange("p (m t) -> p t m", t=PACK),
         )
         nc.vector.tensor_copy(xsg[1][:], xs_tab[:].indirect(offs_sb[:, cols : 2 * cols]))
+        xg.append(keep.tile([P, BANK], U32, name="xg1", tag="w1s_raw", align_bytes=64))
         nc.vector.tensor_copy(xg[1][:], x_tab[:].bitcast(U32).indirect(offs_sb[:, cols : 2 * cols]))
 
         y_sb = [keep.tile([P, S], F32, name="y%d" % t) for t in range(PACK)]
@@ -119,13 +131,15 @@ def tile_picked_yhnswp_rel_p_kernel(
                     start=True,
                     stop=True,
                 )
+                if (t, h) in units[:LEAD]:
+                    nc.vector.tensor_tensor(to_q[:, t, half], acc[:], q_sb[t][:, half], ALU.subtract)
                 nc.scalar.copy(y_sb[t][:, half], acc[:])
                 accs[t, h] = acc
                 if h == 1:
                     nc.sync.dma_start(out=y_twin[t][:], in_=y_sb[t][:])
 
-        def neighbour(t):
-            for h in range(2):
+        def neighbour(t, only=None):
+            for h in range(2) if only is None else [only]:
                 half = slice(h * BANK, (h + 1) * BANK)
                 nc.vector.tensor_tensor(
                     to_n[:, t, half], y_sb[t][:].indirect(hop_sb[:, h * cols : (h + 1) * cols]), y_twin[t][:, half], ALU.subtract
@@ -134,23 +148,26 @@ def tile_picked_yhnswp_rel_p_kernel(
         for t, h in units:
             if True:
                 half = slice(h * BANK, (h + 1) * BANK)
-                nc.vector.tensor_tensor(to_q[:, t, half], accs[t, h][:], q_sb[t][:, half], ALU.subtract)
-                src = to_q[:, t, half].rearrange("p (v d) -> p v d", d=D)
-                if (t, h) in units[-2:]:
-                    nc.vector.tensor_tensor(dq[:, t, h].rearrange("p d v -> p v d"), src, src, ALU.mult)
+                if (t, h) not in units[:LEAD]:
+                    nc.vector.tensor_tensor(to_q[:, t, half], accs[t, h][:], q_sb[t][:, half], ALU.subtract)
+                src = to_q[:, t, half].rearrange("p (w e d) -> p w d e", d=D, e=2)
+                dst = dq[:, t, h].rearrange("p d (w e) -> p w d e", e=2)
+                if (t, h) in units[8 - NSQ :]:
+                    nc.vector.tensor_tensor(dst, src, src, ALU.mult)
                 else:
-                    nc.scalar.activation(dq[:, t, h].rearrange("p d v -> p v d"), src, ACT.Square)
+                    nc.scalar.activation(dst, src, ACT.Square)
         for t, h in units:
             if True:
                 turned = bank(t, h, [P, D, P], "dq_turned")
                 for d in range(D):
                     turn(turned[:, d, :], [dq[:, t, h, d, :]])
                 nc.scalar.activation(root[t][:, (1 - h) * BANK : (2 - h) * BANK], turned[:].rearrange("p d i -> p (d i)"), ACT.Sqrt, bias=0.05)
+        neighbour(0)
         for t in range(PACK):
             nc.vector.tensor_tensor(pairs[:, t], dq[:, t, :, 0:2, :], dq[:, t, :, 2:4, :], ALU.min)
             if t > 0:
                 nc.vector.tensor_tensor(decay[:, t - 1, :, 0:P], pairs[:, t - 1, :, 0, :], pairs[:, t - 1, :, 1, :], ALU.min)
-        neighbour(0)
+        neighbour(1, 0)
         nc.vector.tensor_tensor(decay[:, 3, :, 0:P], pairs[:, 3, :, 0, :], pairs[:, 3, :, 1, :], ALU.min)
         best = decay[:, :, :, 0:P].rearrange("p t h v -> p (t h) v")
         inv_units = inv[:].rearrange("p t (h v) -> p (t h) v", h=2)
@@ -166,9 +183,13 @@ def tile_picked_yhnswp_rel_p_kernel(
             for h in range(2):
                 src = to_n[:, t, h * BANK : (h + 1) * BANK].rearrange("p (v d) -> p v d", d=D)
                 nc.vector.scalar_tensor_tensor(ndn[:, t, h].rearrange("p d v -> p v d"), src, -1.25, src, ALU.mult, ALU.mult)
-                gaps[t, h] = bank(t, h, [P, D, P], "gap")
-                for d in range(D):
-                    turn(gaps[t, h][:, d, :], [dq[:, t, h, d, :], ndn[:, t, h, d, :]])
+                if not PRE:
+                    gaps[t, h] = bank(t, h, [P, D, P], "gap")
+                    for d in range(D):
+                        turn(gaps[t, h][:, d, :], [dq[:, t, h, d, :], ndn[:, t, h, d, :]])
+                else:
+                    for d in range(D):
+                        nc.tensor.matmul(gaps[t, h][:, d, :], ndn[:, t, h, d, :], ident[:], start=False, stop=(d == D - 1), is_transpose=True)
 
         def pick(t, r, on_vector):
             window = windows[t][:].indirect(cand_sb[:, r * rcols : (r + 1) * rcols])
@@ -177,9 +198,14 @@ def tile_picked_yhnswp_rel_p_kernel(
             else:
                 nc.scalar.activation(picked_all[r][:, t, :], window, ACT.Copy)
 
+        if PRE:
+            for t, h in units:
+                gaps[t, h] = bank(t, h, [P, D, P], "gap")
+                for d in range(D):
+                    nc.tensor.matmul(gaps[t, h][:, d, :], dq[:, t, h, d, :], ident[:], start=(d == 0), stop=False, is_transpose=True)
         gap(0)
         for t in range(1, PACK):
-            neighbour(t)
+            neighbour(t, 1 if t == 1 else None)
             gap(t)
         windows = root[1:] + [kd[PACK - 1]]
 
@@ -195,8 +221,12 @@ def tile_picked_yhnswp_rel_p_kernel(
             ranks = []
             for h in range(2):
                 half = slice(h * BANK, (h + 1) * BANK)
-                nc.scalar.activation(root[t][:, (1 - h) * BANK : (2 - h) * BANK], gaps[t, h][:].rearrange("p d i -> p (d i)"), ACT.Tanh, scale=-0.6)
-                nc.vector.scalar_tensor_tensor(kd[t][:, half], root[t][:, (1 - h) * BANK : (2 - h) * BANK], 1.0, decay[:, t, h, :], ALU.add, ALU.mult)
+                pieces = 2 if (SPLIT and (t, h) == (3, 1)) else 1
+                kept = root[t][:, (1 - h) * BANK : (2 - h) * BANK]
+                for c in range(pieces):
+                    cs = slice(c * BANK // pieces, (c + 1) * BANK // pieces)
+                    nc.scalar.activation(kept[:, cs], gaps[t, h][:].rearrange("p d i -> p (d i)")[:, cs], ACT.Tanh, scale=-0.6)
+                    nc.vector.scalar_tensor_tensor(kd[t][:, half][:, cs], kept[:, cs], 1.0, decay[:, t, h, cs], ALU.add, ALU.mult)
                 ranks.append(bank(t, h, [P, P], "rank"))
                 turn(ranks[h][:], [kd[t][:, h * BANK + d * P : h * BANK + (d + 1) * P] for d in range(D)])
             if t > 0:
@@ -205,18 +235,24 @@ def tile_picked_yhnswp_rel_p_kernel(
         ratio(PACK - 1, last)
         for t in range(PACK):
             for r in range(2):
-                pick(t, r, t >= 2 and r == 0)
+                pick(t, r, (t, r) in VP)
 
-        for r in range(2):
-            hid = keep.tile([P, U // 2, PACK], BF16, name="hid%d" % r, align_bytes=64)
-            codes = keep.tile([P, U // 2], U32, name="codes%d" % r, align_bytes=64)
-            hs = keep.tile([P, U // 2], U8, name="hs%d" % r, align_bytes=64)
-            nc.vector.tensor_copy(out=hid[:], in_=picked_all[r][:].rearrange("p t r -> p r t"))
+        width = U // RC
+        for c in range(RC):
+            r, lo = divmod(c * width, U // 2)
+            hid = keep.tile([P, width, PACK], BF16, name="hid%d" % c, align_bytes=64)
+            codes = keep.tile([P, width], U32, name="codes%d" % c, align_bytes=64)
+            hs = keep.tile([P, width], U8, name="hs%d" % c, align_bytes=64)
+            src = picked_all[r][:, :, lo : lo + width].rearrange("p t r -> p r t")
+            if c in SIL:
+                nc.scalar.copy(hid[:], src)
+            else:
+                nc.vector.tensor_copy(out=hid[:], in_=src)
             nc.vector.quantize_mx(out=codes[:].bitcast(FP8X4), scales=hs[:], in_=hid[:].rearrange("p r t -> p (r t)"))
+            acc = bank(c, 0, [P, 2, width], "acc2")
             for a in range(2):
-                acc = psum.tile([P, U // 2], F32, name="acc2", tag="bank%d" % (2 * r + a))
                 nc.tensor.matmul_mx(
-                    out=acc[:],
+                    out=acc[:, a, :],
                     lhsT=w2_sb[:, 2 * P * a : 2 * P * (a + 1)].bitcast(FP4X4),
                     lhsT_scale=w2s_sb[:, P * a : P * (a + 1)],
                     rhs=codes[:].bitcast(FP8X4),
@@ -224,13 +260,6 @@ def tile_picked_yhnswp_rel_p_kernel(
                     start=True,
                     stop=True,
                 )
-                res = keep.tile([P, U // 2], F32, name="res%d_%d" % (r, a))
-                dst = out[a * P : (a + 1) * P, r * (U // 2) : (r + 1) * (U // 2)]
-                if r == 1 and a == 1:
-                    nc.vector.tensor_copy(res[:], acc[:])
-                else:
-                    nc.scalar.copy(res[:], acc[:])
-                if r == 1 and a == 0:
-                    nc.scalar.dma_start(out=dst, in_=res[:])
-                else:
-                    nc.sync.dma_start(out=dst, in_=res[:])
+            res = keep.tile([P, 2, width], F32, name="res%d" % c)
+            nc.scalar.copy(res[:], acc[:])
+            (nc.scalar if c == RC - 1 else nc.sync).dma_start(out=out.rearrange("(a p) r -> p a r", p=P)[:, :, c * width : (c + 1) * width], in_=res[:])

@@ -18,14 +18,16 @@ P = 128
 PACK = 4
 T, S, H, N, V, U, D = 2048, 1024, 512, 256, 256, 512, 4
 BANK = 512
-NSQ = 1
+NSQ = 0
 WARM = 1
-VP = ((2, 0), (3, 0))
+VP = ((3, 0),)
 SIL = (2, 3)
 SPLIT = 1
 LEAD = 0
 RC = 4
 PRE = 1
+NG = 3
+GD = 1
 FLOPS = 2 * 512 * H * S + 2 * H * N * U
 
 
@@ -80,7 +82,7 @@ def tile_picked_yhnswp_rel_p_kernel(
         nc.sync.dma_start(out=w2_sb[:].bitcast(I32), in_=w2_words[0].bitcast(I32))
         load_scale_rows(nc, w2s_sb, w2_scales)
 
-        nc.vector.tensor_copy(
+        (nc.gpsimd if GD else nc.vector).tensor_copy(
             out=w1_sb[:].rearrange("p (t m b) -> p t m b", t=PACK, b=2),
             in_=w1_raw[:].rearrange("p (m t b) -> p t m b", t=PACK, b=2),
         )
@@ -89,28 +91,34 @@ def tile_picked_yhnswp_rel_p_kernel(
         cols = BANK // 16
         nc.vector.tensor_copy(xsg[0][:], xs_tab[:].indirect(offs_sb[:, 0:cols]))
         nc.vector.tensor_copy(xg[0][:], x_tab[:].bitcast(U32).indirect(offs_sb[:, 0:cols]))
-        nc.vector.tensor_copy(
+        (nc.gpsimd if GD else nc.vector).tensor_copy(
             out=w1s_sb[:].rearrange("p (t m) -> p t m", t=PACK),
             in_=w1s_raw[:].rearrange("p (m t) -> p t m", t=PACK),
         )
         nc.vector.tensor_copy(xsg[1][:], xs_tab[:].indirect(offs_sb[:, cols : 2 * cols]))
-        xg.append(keep.tile([P, BANK], U32, name="xg1", tag="w1s_raw", align_bytes=64))
+        xg.append(keep.tile([P, BANK], U32, name="xg1", tag="xg1" if GD else "w1s_raw", align_bytes=64))
         nc.vector.tensor_copy(xg[1][:], x_tab[:].bitcast(U32).indirect(offs_sb[:, cols : 2 * cols]))
 
         y_sb = [keep.tile([P, S], F32, name="y%d" % t) for t in range(PACK)]
         y_twin = [keep.tile([P, S], F32, name="ytwin%d" % t) for t in range(PACK)]
         to_q = keep.tile([P, PACK, S], F32, name="to_q")
         to_n = keep.tile([P, PACK, S], F32, name="to_n")
-        dq = keep.tile([P, PACK, 2, D, P], F32, name="dq")
-        ndn = keep.tile([P, PACK, 2, D, P], F32, name="ndn")
+        dq = keep.tile([P, PACK, 2, V, 2], F32, name="dq")
+        ndn = keep.tile([P, PACK, 2, V, 2], F32, name="ndn")
         root = [keep.tile([P, S], F32, name="root%d" % t) for t in range(PACK)]
         decay = keep.tile([P, PACK, 2, BANK], F32, name="decay")
         kd = [keep.tile([P, S], F32, name="kd%d" % t) for t in range(PACK)]
         inv = keep.tile([P, PACK, V], F32, name="inv")
-        pairs = keep.tile([P, PACK, 2, 2, P], F32, name="pairs")
+        pairs = keep.tile([P, PACK, V, 2], F32, name="pairs")
 
         def bank(t, h, shape, name):
             return psum.tile(shape, F32, name=name, tag="bank%d" % (2 * t + h))
+
+        def member(squares, t, h, d):
+            return squares[:, t, d // 2, h * P : (h + 1) * P, d % 2]
+
+        def by_half(ap):
+            return ap.rearrange("p (h v) -> p h v", h=2)
 
         def turn(dst, sources):
             for n, src in enumerate(sources):
@@ -150,9 +158,11 @@ def tile_picked_yhnswp_rel_p_kernel(
                 half = slice(h * BANK, (h + 1) * BANK)
                 if (t, h) not in units[:LEAD]:
                     nc.vector.tensor_tensor(to_q[:, t, half], accs[t, h][:], q_sb[t][:, half], ALU.subtract)
-                src = to_q[:, t, half].rearrange("p (w e d) -> p w d e", d=D, e=2)
-                dst = dq[:, t, h].rearrange("p d (w e) -> p w d e", e=2)
-                if (t, h) in units[8 - NSQ :]:
+                src = to_q[:, t, half].rearrange("p (v a b) -> p a v b", a=2, b=2)
+                dst = dq[:, t, :, h * P : (h + 1) * P, :]
+                if (t, h) in units[:NG]:
+                    nc.gpsimd.tensor_tensor(dst, src, src, ALU.mult)
+                elif (t, h) in units[8 - NSQ :]:
                     nc.vector.tensor_tensor(dst, src, src, ALU.mult)
                 else:
                     nc.scalar.activation(dst, src, ACT.Square)
@@ -160,15 +170,15 @@ def tile_picked_yhnswp_rel_p_kernel(
             if True:
                 turned = bank(t, h, [P, D, P], "dq_turned")
                 for d in range(D):
-                    turn(turned[:, d, :], [dq[:, t, h, d, :]])
+                    turn(turned[:, d, :], [member(dq, t, h, d)])
                 nc.scalar.activation(root[t][:, (1 - h) * BANK : (2 - h) * BANK], turned[:].rearrange("p d i -> p (d i)"), ACT.Sqrt, bias=0.05)
         neighbour(0)
         for t in range(PACK):
-            nc.vector.tensor_tensor(pairs[:, t], dq[:, t, :, 0:2, :], dq[:, t, :, 2:4, :], ALU.min)
+            nc.vector.tensor_tensor(pairs[:, t], dq[:, t, 0], dq[:, t, 1], ALU.min)
             if t > 0:
-                nc.vector.tensor_tensor(decay[:, t - 1, :, 0:P], pairs[:, t - 1, :, 0, :], pairs[:, t - 1, :, 1, :], ALU.min)
+                nc.vector.tensor_tensor(decay[:, t - 1, :, 0:P], by_half(pairs[:, t - 1, :, 0]), by_half(pairs[:, t - 1, :, 1]), ALU.min)
         neighbour(1, 0)
-        nc.vector.tensor_tensor(decay[:, 3, :, 0:P], pairs[:, 3, :, 0, :], pairs[:, 3, :, 1, :], ALU.min)
+        nc.vector.tensor_tensor(decay[:, 3, :, 0:P], by_half(pairs[:, 3, :, 0]), by_half(pairs[:, 3, :, 1]), ALU.min)
         best = decay[:, :, :, 0:P].rearrange("p t h v -> p (t h) v")
         inv_units = inv[:].rearrange("p t (h v) -> p (t h) v", h=2)
         nc.scalar.activation(inv_units, best, ACT.Ln, bias=1.0, scale=2.0)
@@ -180,16 +190,17 @@ def tile_picked_yhnswp_rel_p_kernel(
         gaps = {}
 
         def gap(t):
+            for a in range(2):
+                src = to_n[:, t, :].rearrange("p (v a b) -> p a v b", a=2, b=2)[:, a]
+                nc.vector.scalar_tensor_tensor(ndn[:, t, a], src, -1.25, src, ALU.mult, ALU.mult)
             for h in range(2):
-                src = to_n[:, t, h * BANK : (h + 1) * BANK].rearrange("p (v d) -> p v d", d=D)
-                nc.vector.scalar_tensor_tensor(ndn[:, t, h].rearrange("p d v -> p v d"), src, -1.25, src, ALU.mult, ALU.mult)
                 if not PRE:
                     gaps[t, h] = bank(t, h, [P, D, P], "gap")
                     for d in range(D):
-                        turn(gaps[t, h][:, d, :], [dq[:, t, h, d, :], ndn[:, t, h, d, :]])
+                        turn(gaps[t, h][:, d, :], [member(dq, t, h, d), member(ndn, t, h, d)])
                 else:
                     for d in range(D):
-                        nc.tensor.matmul(gaps[t, h][:, d, :], ndn[:, t, h, d, :], ident[:], start=False, stop=(d == D - 1), is_transpose=True)
+                        nc.tensor.matmul(gaps[t, h][:, d, :], member(ndn, t, h, d), ident[:], start=False, stop=(d == D - 1), is_transpose=True)
 
         def pick(t, r, on_vector):
             window = windows[t][:].indirect(cand_sb[:, r * rcols : (r + 1) * rcols])
@@ -202,7 +213,7 @@ def tile_picked_yhnswp_rel_p_kernel(
             for t, h in units:
                 gaps[t, h] = bank(t, h, [P, D, P], "gap")
                 for d in range(D):
-                    nc.tensor.matmul(gaps[t, h][:, d, :], dq[:, t, h, d, :], ident[:], start=(d == 0), stop=False, is_transpose=True)
+                    nc.tensor.matmul(gaps[t, h][:, d, :], member(dq, t, h, d), ident[:], start=(d == 0), stop=False, is_transpose=True)
         gap(0)
         for t in range(1, PACK):
             neighbour(t, 1 if t == 1 else None)

@@ -20,7 +20,7 @@ T, S, H, N, V, U, D = 2048, 1024, 512, 256, 256, 512, 4
 BANK = 512
 NSQ = 0
 WARM = 1
-VP = ((3, 0),)
+VP = ((0, 0), (3, 0))
 SIL = (2, 3)
 SPLIT = 1
 LEAD = 0
@@ -28,6 +28,10 @@ RC = 4
 PRE = 1
 NG = 3
 GD = 1
+NT = (3,)
+SQD = 1
+AFT = 1
+EARLY = (3,)
 FLOPS = 2 * 512 * H * S + 2 * H * N * U
 
 
@@ -120,6 +124,13 @@ def tile_picked_yhnswp_rel_p_kernel(
         def by_half(ap):
             return ap.rearrange("p (h v) -> p h v", h=2)
 
+        def flat(squares, t, h):
+            return squares[:, t, :, h * P : (h + 1) * P, :].rearrange("p a v b -> p a (v b)")
+
+        def root_half(t, h):
+            slot = h if t in EARLY else 1 - h
+            return root[t][:, slot * BANK : (slot + 1) * BANK]
+
         def turn(dst, sources):
             for n, src in enumerate(sources):
                 nc.tensor.matmul(dst, src, ident[:], start=(n == 0), stop=(n == len(sources) - 1), is_transpose=True)
@@ -168,10 +179,13 @@ def tile_picked_yhnswp_rel_p_kernel(
                     nc.scalar.activation(dst, src, ACT.Square)
         for t, h in units:
             if True:
+                if t in NT:
+                    nc.scalar.activation(by_half(root_half(t, h)), flat(dq, t, h), ACT.Sqrt, bias=0.05)
+                    continue
                 turned = bank(t, h, [P, D, P], "dq_turned")
                 for d in range(D):
                     turn(turned[:, d, :], [member(dq, t, h, d)])
-                nc.scalar.activation(root[t][:, (1 - h) * BANK : (2 - h) * BANK], turned[:].rearrange("p d i -> p (d i)"), ACT.Sqrt, bias=0.05)
+                nc.scalar.activation(root_half(t, h), turned[:].rearrange("p d i -> p (d i)"), ACT.Sqrt, bias=0.05)
         neighbour(0)
         for t in range(PACK):
             nc.vector.tensor_tensor(pairs[:, t], dq[:, t, 0], dq[:, t, 1], ALU.min)
@@ -190,11 +204,20 @@ def tile_picked_yhnswp_rel_p_kernel(
         gaps = {}
 
         def gap(t):
+            if t in NT and SQD:
+                for h in range(2):
+                    src = to_n[:, t, h * BANK : (h + 1) * BANK].rearrange("p (v a b) -> p a v b", a=2, b=2)
+                    dn = decay[:, 0, h, :]
+                    nc.scalar.activation(dn.rearrange("p (a v b) -> p a v b", a=2, b=2), src, ACT.Square)
+                    nc.vector.scalar_tensor_tensor(flat(ndn, t, h), by_half(dn), -1.25, flat(dq, t, h), ALU.mult, ALU.add)
+                return
             for a in range(2):
                 src = to_n[:, t, :].rearrange("p (v a b) -> p a v b", a=2, b=2)[:, a]
                 nc.vector.scalar_tensor_tensor(ndn[:, t, a], src, -1.25, src, ALU.mult, ALU.mult)
             for h in range(2):
-                if not PRE:
+                if t in NT:
+                    nc.vector.tensor_tensor(flat(ndn, t, h), flat(ndn, t, h), flat(dq, t, h), ALU.add)
+                elif not PRE:
                     gaps[t, h] = bank(t, h, [P, D, P], "gap")
                     for d in range(D):
                         turn(gaps[t, h][:, d, :], [member(dq, t, h, d), member(ndn, t, h, d)])
@@ -211,13 +234,16 @@ def tile_picked_yhnswp_rel_p_kernel(
 
         if PRE:
             for t, h in units:
+                if t in NT:
+                    continue
                 gaps[t, h] = bank(t, h, [P, D, P], "gap")
                 for d in range(D):
                     nc.tensor.matmul(gaps[t, h][:, d, :], member(dq, t, h, d), ident[:], start=(d == 0), stop=False, is_transpose=True)
         gap(0)
         for t in range(1, PACK):
             neighbour(t, 1 if t == 1 else None)
-            gap(t)
+            if t not in NT:
+                gap(t)
         windows = root[1:] + [kd[PACK - 1]]
 
         def ratio(t, ranks):
@@ -228,21 +254,33 @@ def tile_picked_yhnswp_rel_p_kernel(
         last = None
         for t in range(PACK):
             for h in range(2):
-                nc.scalar.activation(decay[:, t, h, :], root[t][:, (1 - h) * BANK : (2 - h) * BANK], ACT.Exp, scale=-1.0)
+                nc.scalar.activation(decay[:, t, h, :], root_half(t, h), ACT.Exp, scale=-1.0)
             ranks = []
             for h in range(2):
                 half = slice(h * BANK, (h + 1) * BANK)
                 pieces = 2 if (SPLIT and (t, h) == (3, 1)) else 1
-                kept = root[t][:, (1 - h) * BANK : (2 - h) * BANK]
+                kept = root_half(t, h)
+                if t in NT:
+                    nc.scalar.activation(by_half(kept), flat(ndn, t, h), ACT.Tanh, scale=-0.6)
+                    nc.vector.scalar_tensor_tensor(kd[t][:, half], kept, 1.0, decay[:, t, h, :], ALU.add, ALU.mult)
+                    if h == 0 and t in EARLY:
+                        ratio(t - 1, last)
+                    two = pairs[:, t, h * P : (h + 1) * P, :]
+                    nc.vector.tensor_tensor(two.rearrange("p v b -> p (v b)"), kd[t][:, h * BANK : h * BANK + V], kd[t][:, h * BANK + V : (h + 1) * BANK], ALU.add)
+                    ranks.append(keep.tile([P, P], F32, name="rank%d_%d" % (t, h)))
+                    nc.vector.tensor_tensor(ranks[h][:], two[:, :, 0], two[:, :, 1], ALU.add)
+                    continue
                 for c in range(pieces):
                     cs = slice(c * BANK // pieces, (c + 1) * BANK // pieces)
                     nc.scalar.activation(kept[:, cs], gaps[t, h][:].rearrange("p d i -> p (d i)")[:, cs], ACT.Tanh, scale=-0.6)
                     nc.vector.scalar_tensor_tensor(kd[t][:, half][:, cs], kept[:, cs], 1.0, decay[:, t, h, cs], ALU.add, ALU.mult)
                 ranks.append(bank(t, h, [P, P], "rank"))
                 turn(ranks[h][:], [kd[t][:, h * BANK + d * P : h * BANK + (d + 1) * P] for d in range(D)])
-            if t > 0:
+            if t > 0 and t not in EARLY:
                 ratio(t - 1, last)
             last = ranks
+            if t == AFT:
+                gap(NT[0])
         ratio(PACK - 1, last)
         for t in range(PACK):
             for r in range(2):

from contextlib import ExitStack

import concourse.mybir as mybir
from concourse.masks import make_identity

F32 = mybir.dt.float32
BF16 = mybir.dt.bfloat16
I32 = mybir.dt.int32
U32 = mybir.dt.uint32
U16 = mybir.dt.uint16
U8 = mybir.dt.uint8
FP8X4 = mybir.dt.float8_e4m3fn_x4
FP4X4 = mybir.dt.float4_e2m1fn_x4
ALU = mybir.AluOpType
ACT = mybir.ActivationFunctionType

P = 128
PACK = 4
T, S, H, N, V, U, D = 2048, 1024, 512, 256, 256, 512, 4
BANK = 512
NSQ = 0
WARM = 1
VP = ((0, 0), (3, 0))
SIL = (2, 3)
SPLIT = 1
LEAD = 0
RC = 4
PRE = 1
NG = 3
GD = 1
NT = (3,)
SQD = 1
AFT = 1
EARLY = (3,)
FLOPS = 2 * 512 * H * S + 2 * H * N * U


def load_scale_rows(nc, plane, scales):
    for q in range(4):
        nc.sync.dma_start(out=plane[32 * q : 32 * q + 4, :].bitcast(I32), in_=scales[0, 4 * q : 4 * q + 4, :].bitcast(I32))


def tile_picked_yhnswp_rel_p_kernel(
    tc, x_words, x_scales, w1_words, w1_scales, qry, unit, w2_words, w2_scales, offs, hop, cand, out
):
    nc = tc.nc
    with ExitStack() as ctx:
        keep = ctx.enter_context(tc.tile_pool(name="keep", bufs=1))
        psum = ctx.enter_context(tc.psum_pool(name="psum", bufs=1))

        offs_sb = keep.tile([P, S // 16], U16, name="offs_sb")
        hop_sb = keep.tile([P, S // 16], U16, name="hop_sb")
        cand_sb = keep.tile([P, U // 16], U16, name="cand_sb")
        x_tab = keep.tile([P, T], I32, name="x_tab", align_bytes=64)
        xs_tab = keep.tile([P, T], U8, name="xs_tab", align_bytes=64)
        w1_raw = keep.tile([P, 2 * H], U8, name="w1_raw", align_bytes=64)
        w1s_raw = keep.tile([P, H], U8, name="w1s_raw", align_bytes=64)
        w1_sb = keep.tile([P, 2 * H], U8, name="w1_sb", align_bytes=64)
        w1s_sb = keep.tile([P, H], U8, name="w1s_sb", align_bytes=64)
        w2_sb = keep.tile([P, 2 * N], U8, name="w2_sb", align_bytes=64)
        w2s_sb = keep.tile([P, N], U8, name="w2s_sb", align_bytes=64)
        unit_sb = keep.tile([P, PACK], F32, name="unit_sb")
        q_sb = [keep.tile([P, S], F32, name="q%d" % t) for t in range(PACK)]

        nc.gpsimd.memset(xs_tab[:].bitcast(I32), 0)
        nc.gpsimd.memset(w1s_raw[:].bitcast(I32), 0)
        nc.gpsimd.memset(w2s_sb[:].bitcast(I32), 0)

        ident = keep.tile([P, P], F32, name="ident")
        make_identity(nc, ident[:])

        if WARM:
            warm = keep.tile([P, 1], F32, name="warm")
            nc.scalar.activation(warm[:], w2s_sb[:, 0:4].bitcast(F32), ACT.Sqrt)
        nc.sync.dma_start(offs_sb[:], offs)
        nc.sync.dma_start(out=w1_raw[:].bitcast(I32), in_=w1_words[0].bitcast(I32))
        nc.sync.dma_start(hop_sb[:], hop)
        load_scale_rows(nc, xs_tab, x_scales)
        nc.sync.dma_start(out=x_tab[:], in_=x_words[0].rearrange("p n r -> p (n r)").bitcast(I32))
        load_scale_rows(nc, w1s_raw, w1_scales)
        q_rows = qry.rearrange("(p t) j -> p t j", t=PACK)
        for t in range(PACK):
            nc.sync.dma_start(out=q_sb[t][:], in_=q_rows[:, t, :])
        nc.sync.dma_start(cand_sb[:], cand)
        nc.sync.dma_start(out=unit_sb[:], in_=unit.rearrange("(p t) o -> p (t o)", t=PACK))
        nc.sync.dma_start(out=w2_sb[:].bitcast(I32), in_=w2_words[0].bitcast(I32))
        load_scale_rows(nc, w2s_sb, w2_scales)

        (nc.gpsimd if GD else nc.vector).tensor_copy(
            out=w1_sb[:].rearrange("p (t m b) -> p t m b", t=PACK, b=2),
            in_=w1_raw[:].rearrange("p (m t b) -> p t m b", t=PACK, b=2),
        )
        xg = [keep.tile([P, BANK], U32, name="xg0", align_bytes=64)]
        xsg = [keep.tile([P, BANK], U8, name="xsg%d" % h, align_bytes=64) for h in range(2)]
        cols = BANK // 16
        nc.vector.tensor_copy(xsg[0][:], xs_tab[:].indirect(offs_sb[:, 0:cols]))
        nc.vector.tensor_copy(xg[0][:], x_tab[:].bitcast(U32).indirect(offs_sb[:, 0:cols]))
        (nc.gpsimd if GD else nc.vector).tensor_copy(
            out=w1s_sb[:].rearrange("p (t m) -> p t m", t=PACK),
            in_=w1s_raw[:].rearrange("p (m t) -> p t m", t=PACK),
        )
        nc.vector.tensor_copy(xsg[1][:], xs_tab[:].indirect(offs_sb[:, cols : 2 * cols]))
        xg.append(keep.tile([P, BANK], U32, name="xg1", tag="xg1" if GD else "w1s_raw", align_bytes=64))
        nc.vector.tensor_copy(xg[1][:], x_tab[:].bitcast(U32).indirect(offs_sb[:, cols : 2 * cols]))

        y_sb = [keep.tile([P, S], F32, name="y%d" % t) for t in range(PACK)]
        y_twin = [keep.tile([P, S], F32, name="ytwin%d" % t) for t in range(PACK)]
        to_q = keep.tile([P, PACK, S], F32, name="to_q")
        to_n = keep.tile([P, PACK, S], F32, name="to_n")
        dq = keep.tile([P, PACK, 2, V, 2], F32, name="dq")
        ndn = keep.tile([P, PACK, 2, V, 2], F32, name="ndn")
        root = [keep.tile([P, S], F32, name="root%d" % t) for t in range(PACK)]
        decay = keep.tile([P, PACK, 2, BANK], F32, name="decay")
        kd = [keep.tile([P, S], F32, name="kd%d" % t) for t in range(PACK)]
        inv = keep.tile([P, PACK, V], F32, name="inv")
        pairs = keep.tile([P, PACK, V, 2], F32, name="pairs")

        def bank(t, h, shape, name):
            return psum.tile(shape, F32, name=name, tag="bank%d" % (2 * t + h))

        def member(squares, t, h, d):
            return squares[:, t, d // 2, h * P : (h + 1) * P, d % 2]

        def by_half(ap):
            return ap.rearrange("p (h v) -> p h v", h=2)

        def flat(squares, t, h):
            return squares[:, t, :, h * P : (h + 1) * P, :].rearrange("p a v b -> p a (v b)")

        def root_half(t, h):
            slot = h if t in EARLY else 1 - h
            return root[t][:, slot * BANK : (slot + 1) * BANK]

        def turn(dst, sources):
            for n, src in enumerate(sources):
                nc.tensor.matmul(dst, src, ident[:], start=(n == 0), stop=(n == len(sources) - 1), is_transpose=True)

        accs = {}
        units = [(0, 0), (1, 0), (2, 0), (0, 1), (1, 1), (3, 0), (2, 1), (3, 1)]
        for t, h in units:
            half = slice(h * BANK, (h + 1) * BANK)
            if True:
                acc = bank(t, h, [P, BANK], "acc")
                nc.tensor.matmul_mx(
                    out=acc[:],
                    lhsT=w1_sb[:, 2 * P * t : 2 * P * (t + 1)].bitcast(FP4X4),
                    lhsT_scale=w1s_sb[:, P * t : P * (t + 1)],
                    rhs=xg[h][:].bitcast(FP8X4),
                    rhs_scale=xsg[h][:],
                    start=True,
                    stop=True,
                )
                if (t, h) in units[:LEAD]:
                    nc.vector.tensor_tensor(to_q[:, t, half], acc[:], q_sb[t][:, half], ALU.subtract)
                nc.scalar.copy(y_sb[t][:, half], acc[:])
                accs[t, h] = acc
                if h == 1:
                    nc.sync.dma_start(out=y_twin[t][:], in_=y_sb[t][:])

        def neighbour(t, only=None):
            for h in range(2) if only is None else [only]:
                half = slice(h * BANK, (h + 1) * BANK)
                nc.vector.tensor_tensor(
                    to_n[:, t, half], y_sb[t][:].indirect(hop_sb[:, h * cols : (h + 1) * cols]), y_twin[t][:, half], ALU.subtract
                )

        for t, h in units:
            if True:
                half = slice(h * BANK, (h + 1) * BANK)
                if (t, h) not in units[:LEAD]:
                    nc.vector.tensor_tensor(to_q[:, t, half], accs[t, h][:], q_sb[t][:, half], ALU.subtract)
                src = to_q[:, t, half].rearrange("p (v a b) -> p a v b", a=2, b=2)
                dst = dq[:, t, :, h * P : (h + 1) * P, :]
                if (t, h) in units[:NG]:
                    nc.gpsimd.tensor_tensor(dst, src, src, ALU.mult)
                elif (t, h) in units[8 - NSQ :]:
                    nc.vector.tensor_tensor(dst, src, src, ALU.mult)
                else:
                    nc.scalar.activation(dst, src, ACT.Square)
        for t, h in units:
            if True:
                if t in NT:
                    nc.scalar.activation(by_half(root_half(t, h)), flat(dq, t, h), ACT.Sqrt, bias=0.05)
                    continue
                turned = bank(t, h, [P, D, P], "dq_turned")
                for d in range(D):
                    turn(turned[:, d, :], [member(dq, t, h, d)])
                nc.scalar.activation(root_half(t, h), turned[:].rearrange("p d i -> p (d i)"), ACT.Sqrt, bias=0.05)
        neighbour(0)
        for t in range(PACK):
            nc.vector.tensor_tensor(pairs[:, t], dq[:, t, 0], dq[:, t, 1], ALU.min)
            if t > 0:
                nc.vector.tensor_tensor(decay[:, t - 1, :, 0:P], by_half(pairs[:, t - 1, :, 0]), by_half(pairs[:, t - 1, :, 1]), ALU.min)
        neighbour(1, 0)
        nc.vector.tensor_tensor(decay[:, 3, :, 0:P], by_half(pairs[:, 3, :, 0]), by_half(pairs[:, 3, :, 1]), ALU.min)
        best = decay[:, :, :, 0:P].rearrange("p t h v -> p (t h) v")
        inv_units = inv[:].rearrange("p t (h v) -> p (t h) v", h=2)
        nc.scalar.activation(inv_units, best, ACT.Ln, bias=1.0, scale=2.0)
        nc.scalar.activation(inv[:], inv[:], ACT.Exp, scale=-1.0)

        picked_all = [keep.tile([P, PACK, U // 2], BF16, name="pickedall%d" % r, align_bytes=64) for r in range(2)]
        rcols = U // 32

        gaps = {}

        def gap(t):
            if t in NT and SQD:
                for h in range(2):
                    src = to_n[:, t, h * BANK : (h + 1) * BANK].rearrange("p (v a b) -> p a v b", a=2, b=2)
                    dn = decay[:, 0, h, :]
                    nc.scalar.activation(dn.rearrange("p (a v b) -> p a v b", a=2, b=2), src, ACT.Square)
                    nc.vector.scalar_tensor_tensor(flat(ndn, t, h), by_half(dn), -1.25, flat(dq, t, h), ALU.mult, ALU.add)
                return
            for a in range(2):
                src = to_n[:, t, :].rearrange("p (v a b) -> p a v b", a=2, b=2)[:, a]
                nc.vector.scalar_tensor_tensor(ndn[:, t, a], src, -1.25, src, ALU.mult, ALU.mult)
            for h in range(2):
                if t in NT:
                    nc.vector.tensor_tensor(flat(ndn, t, h), flat(ndn, t, h), flat(dq, t, h), ALU.add)
                elif not PRE:
                    gaps[t, h] = bank(t, h, [P, D, P], "gap")
                    for d in range(D):
                        turn(gaps[t, h][:, d, :], [member(dq, t, h, d), member(ndn, t, h, d)])
                else:
                    for d in range(D):
                        nc.tensor.matmul(gaps[t, h][:, d, :], member(ndn, t, h, d), ident[:], start=False, stop=(d == D - 1), is_transpose=True)

        def pick(t, r, on_vector):
            window = windows[t][:].indirect(cand_sb[:, r * rcols : (r + 1) * rcols])
            if on_vector:
                nc.vector.tensor_copy(picked_all[r][:, t, :], window)
            else:
                nc.scalar.activation(picked_all[r][:, t, :], window, ACT.Copy)

        if PRE:
            for t, h in units:
                if t in NT:
                    continue
                gaps[t, h] = bank(t, h, [P, D, P], "gap")
                for d in range(D):
                    nc.tensor.matmul(gaps[t, h][:, d, :], member(dq, t, h, d), ident[:], start=(d == 0), stop=False, is_transpose=True)
        gap(0)
        for t in range(1, PACK):
            neighbour(t, 1 if t == 1 else None)
            if t not in NT:
                gap(t)
        windows = root[1:] + [kd[PACK - 1]]

        def ratio(t, ranks):
            for h in range(2):
                vs = slice(h * P, (h + 1) * P)
                nc.vector.scalar_tensor_tensor(windows[t][:, vs], ranks[h][:], unit_sb[:, t : t + 1], inv[:, t, vs], ALU.mult, ALU.mult)

        last = None
        for t in range(PACK):
            for h in range(2):
                nc.scalar.activation(decay[:, t, h, :], root_half(t, h), ACT.Exp, scale=-1.0)
            ranks = []
            for h in range(2):
                half = slice(h * BANK, (h + 1) * BANK)
                pieces = 2 if (SPLIT and (t, h) == (3, 1)) else 1
                kept = root_half(t, h)
                if t in NT:
                    nc.scalar.activation(by_half(kept), flat(ndn, t, h), ACT.Tanh, scale=-0.6)
                    nc.vector.scalar_tensor_tensor(kd[t][:, half], kept, 1.0, decay[:, t, h, :], ALU.add, ALU.mult)
                    if h == 0 and t in EARLY:
                        ratio(t - 1, last)
                    two = pairs[:, t, h * P : (h + 1) * P, :]
                    nc.vector.tensor_tensor(two.rearrange("p v b -> p (v b)"), kd[t][:, h * BANK : h * BANK + V], kd[t][:, h * BANK + V : (h + 1) * BANK], ALU.add)
                    ranks.append(keep.tile([P, P], F32, name="rank%d_%d" % (t, h)))
                    nc.vector.tensor_tensor(ranks[h][:], two[:, :, 0], two[:, :, 1], ALU.add)
                    continue
                for c in range(pieces):
                    cs = slice(c * BANK // pieces, (c + 1) * BANK // pieces)
                    nc.scalar.activation(kept[:, cs], gaps[t, h][:].rearrange("p d i -> p (d i)")[:, cs], ACT.Tanh, scale=-0.6)
                    nc.vector.scalar_tensor_tensor(kd[t][:, half][:, cs], kept[:, cs], 1.0, decay[:, t, h, cs], ALU.add, ALU.mult)
                ranks.append(bank(t, h, [P, P], "rank"))
                turn(ranks[h][:], [kd[t][:, h * BANK + d * P : h * BANK + (d + 1) * P] for d in range(D)])
            if t > 0 and t not in EARLY:
                ratio(t - 1, last)
            last = ranks
            if t == AFT:
                gap(NT[0])
        ratio(PACK - 1, last)
        for t in range(PACK):
            for r in range(2):
                pick(t, r, (t, r) in VP)

        width = U // RC
        for c in range(RC):
            r, lo = divmod(c * width, U // 2)
            hid = keep.tile([P, width, PACK], BF16, name="hid%d" % c, align_bytes=64)
            codes = keep.tile([P, width], U32, name="codes%d" % c, align_bytes=64)
            hs = keep.tile([P, width], U8, name="hs%d" % c, align_bytes=64)
            src = picked_all[r][:, :, lo : lo + width].rearrange("p t r -> p r t")
            if c in SIL:
                nc.scalar.copy(hid[:], src)
            else:
                nc.vector.tensor_copy(out=hid[:], in_=src)
            nc.vector.quantize_mx(out=codes[:].bitcast(FP8X4), scales=hs[:], in_=hid[:].rearrange("p r t -> p (r t)"))
            acc = bank(c, 0, [P, 2, width], "acc2")
            for a in range(2):
                nc.tensor.matmul_mx(
                    out=acc[:, a, :],
                    lhsT=w2_sb[:, 2 * P * a : 2 * P * (a + 1)].bitcast(FP4X4),
                    lhsT_scale=w2s_sb[:, P * a : P * (a + 1)],
                    rhs=codes[:].bitcast(FP8X4),
                    rhs_scale=hs[:],
                    start=True,
                    stop=True,
                )
            res = keep.tile([P, 2, width], F32, name="res%d" % c)
            nc.scalar.copy(res[:], acc[:])
            (nc.scalar if c == RC - 1 else nc.sync).dma_start(out=out.rearrange("(a p) r -> p a r", p=P)[:, :, c * width : (c + 1) * width], in_=res[:])
